import numpy as np
import ml_dtypes


def mxq(x, axis, fmt="e4m3"):
    dtype, down = {"e4m3": (ml_dtypes.float8_e4m3fn, 7), "e5m2": (ml_dtypes.float8_e5m2, 14)}[fmt]
    v = np.moveaxis(np.asarray(x, np.float32).astype(ml_dtypes.bfloat16).astype(np.float64), axis, -1)
    blocks = v.reshape(v.shape[:-1] + (-1, 32))
    amax = np.abs(blocks).max(-1, keepdims=True)
    byte = np.maximum(np.where(amax > 0, np.frexp(amax)[1] - 1 + 127, 0) - down, 1)
    scale = np.exp2(byte - 127.0)
    codes = (blocks / scale).astype(np.float32).astype(dtype).astype(np.float64)
    return np.moveaxis((codes * scale).reshape(v.shape), -1, axis)


WIDE = False


def mx_kscale(k):
    if not WIDE:
        return np.ones(k)
    levels = np.array([10, -10, 5, -5, 0])
    if k % 512:
        return np.exp2(np.random.permutation(np.resize(levels, k // 32))).repeat(32)
    a = np.empty((k // 512, 16))
    for p in range(k // 512):
        a[p, :8] = np.random.permutation(np.resize(levels, 8))
        for g in range(8):
            far = levels[np.abs(levels - a[p, g]) >= 10]
            a[p, g + 8] = far[np.random.randint(len(far))]
    return np.exp2(a.ravel()).repeat(32)


BF16 = ml_dtypes.bfloat16


def bf(x):
    return np.asarray(x, np.float32).astype(BF16)


def f64(x):
    return np.asarray(x).astype(np.float64)


E2M1 = np.array([0.0, 0.5, 1.0, 1.5, 2.0, 3.0, 4.0, 6.0, -0.0, -0.5, -1.0, -1.5, -2.0, -3.0, -4.0, -6.0])


def pack_weight(w, fmt):
    k, n = w.shape
    w = f64(bf(w)).reshape(k // 32, 32, n)
    amax = np.abs(w).max(1)
    if fmt == "e4m3":
        byte = np.frexp(amax)[1] - 1 + 127 - 7
    else:
        mant, ex = np.frexp(amax / 6.0)
        byte = np.where(mant > 0.5, ex, ex - 1) + 127
    byte = np.clip(np.where(amax > 0, byte, 1), 1, 254)
    scaled = (w * np.exp2(127.0 - byte)[:, None, :]).reshape(k, n).astype(np.float32)
    by_word = np.ascontiguousarray(scaled.reshape(k // 512, 128, 4, n).transpose(0, 1, 3, 2))
    if fmt == "e4m3":
        words = by_word.astype(ml_dtypes.float8_e4m3fn).view(np.uint8)
    else:
        c = by_word.astype(ml_dtypes.float4_e2m1fn).view(np.uint8) & 0xF
        words = c[..., 0::2] | (c[..., 1::2] << 4)
    return np.ascontiguousarray(words), np.ascontiguousarray(byte.astype(np.uint8).reshape(k // 512, 16, n))


def unpack_weight(words, scales, fmt):
    g, p, n, _ = words.shape
    if fmt == "e4m3":
        vals = np.ascontiguousarray(words).view(ml_dtypes.float8_e4m3fn).astype(np.float64)
    else:
        nib = np.empty((g, p, n, 4), np.uint8)
        nib[..., 0::2] = words & 0xF
        nib[..., 1::2] = words >> 4
        vals = E2M1[nib]
    vals = vals * np.repeat(np.exp2(scales.astype(np.float64) - 127.0), 8, axis=1)[..., None]
    return vals.transpose(0, 1, 3, 2).reshape(g * 512, n)
def pack4(w):
    words, scales = pack_weight(w, "e2m1")
    return words.reshape(words.shape[0], 128, -1), scales


def unpack4(words, scales):
    return unpack_weight(words.reshape(words.shape[0], 128, -1, 2), scales, "e2m1")


def planes(Y):
    n, m = Y.shape
    b = f64(bf(Y)).reshape(n // 32, 32, m)
    amax = np.abs(b).max(1)
    byte = np.clip(np.where(amax > 0, np.frexp(amax)[1] - 1 + 127 - 7, 1), 1, 254)
    codes = (b * np.exp2(127.0 - byte)[:, None, :]).reshape(n, m).astype(np.float32).astype(ml_dtypes.float8_e4m3fn).view(np.uint8)
    words = codes.reshape(n // 512, 128, 4, m).transpose(0, 1, 3, 2)
    return np.ascontiguousarray(words), np.ascontiguousarray(byte.astype(np.uint8).reshape(n // 512, 16, m))


L, D, G, Q = 1024, 512, 1536, 1024


def setup_inputs():
    sd, sg = mx_kscale(D), mx_kscale(G)
    u = bf(np.random.standard_normal((L, D)) * sd[None, :])
    v_words, v_scales = pack4(np.random.standard_normal((D, G)) / np.sqrt(D) / sd[:, None])
    b = bf(np.random.standard_normal(G) * 0.5)
    t = bf(np.random.uniform(0.5, 1.5, L))
    p = bf(np.random.uniform(0.3, 1.0, G) * sg)
    a_words, a_scales = pack4(2.0 * np.random.standard_normal((G, Q)) / np.sqrt(G) / sg[:, None])
    c = bf(np.random.standard_normal(L) * 0.5)
    return {"u": u,
            "v_words": v_words,
            "v_scales": v_scales,
            "b": b,
            "t": t,
            "p": p,
            "a_words": a_words,
            "a_scales": a_scales,
            "c": c}


def growth_rate_change(u, v, b):
    s = mxq(u, 1, "e4m3") @ v
    return 0.4 * (s + b[None, :])


def core(u, v_words, v_scales, b, t, p, a_words, a_scales, c):
    rate = growth_rate_change(f64(u), unpack4(v_words, v_scales), f64(b))
    x = np.exp(f64(t)[:, None] * rate) - 1.0
    m = f64(p)[None, :] * x
    f = mxq(m, 1, "e4m3") @ unpack4(a_words, a_scales)
    return f + f64(c)[:, None]


def reference(u, v_words, v_scales, b, t, p, a_words, a_scales, c):
    R_out = core(u, v_words, v_scales, b, t, p, a_words, a_scales, c)
    words, scales = planes(R_out.T)
    return R_out, words, scales

@@ -1,0 +1,365 @@
+from contextlib import ExitStack
+
+import concourse.mybir as mybir
+from concourse.masks import make_identity
+
+L, D, G, Q = 1024, 512, 1536, 1024
+FLOPS = 2 * L * D * G + 2 * L * G * Q
+
+F32 = mybir.dt.float32
+BF16 = mybir.dt.bfloat16
+U32 = mybir.dt.uint32
+I32 = mybir.dt.int32
+U8 = mybir.dt.uint8
+E4X4 = mybir.dt.float8_e4m3fn_x4
+E2X4 = mybir.dt.float4_e2m1fn_x4
+ADD = mybir.AluOpType.add
+MULT = mybir.AluOpType.mult
+EXP = mybir.ActivationFunctionType.Exp
+IDENT = mybir.ActivationFunctionType.Identity
+
+P = 128
+PACK = 4
+GP = G // 512
+QG = Q // 512
+CHUNKS = (128, 256, 256, 256, 128)
+
+
+def tile_knockoutpopulationgrowthguidereadout_x2_kernel(
+    tc, u, v_words, v_scales, b, t, p, a_words, a_scales, c, out_0, out_1, out_2
+):
+    nc = tc.nc
+    starts = [sum(CHUNKS[:i]) for i in range(len(CHUNKS))]
+    units = [(ci, g) for ci in range(len(CHUNKS)) for g in range(GP)]
+
+    with ExitStack() as ctx:
+        keep = ctx.enter_context(tc.tile_pool(name="keep", bufs=1))
+        work = ctx.enter_context(tc.tile_pool(name="work", bufs=3))
+        psum = ctx.enter_context(tc.psum_pool(name="psum", bufs=2))
+        ctx.enter_context(tc.manual_schedule())
+
+        ident = keep.tile([P, P], F32, name="ident", align_bytes=64)
+        ident_bf = keep.tile([P, P], BF16, name="ident_bf", align_bytes=64)
+        v_raw = keep.tile([P, 2 * G], U8, name="v_raw", align_bytes=64)
+        vs_raw = keep.tile([P, G], U8, name="vs_raw", align_bytes=64)
+        v_perm = keep.tile([P, GP, PACK, 2 * P], U8, name="v_perm", align_bytes=64)
+        vs_perm = keep.tile([P, GP, PACK, P], U8, name="vs_perm", align_bytes=64)
+        a_sb = keep.tile([P, GP, 2 * Q], U8, name="a_sb", align_bytes=64)
+        as_sb = keep.tile([P, GP * Q], U8, name="as_sb", align_bytes=64)
+        b_sb = keep.tile([P, GP, PACK], BF16, name="b_sb", align_bytes=64)
+        p_sb = keep.tile([P, GP, PACK], BF16, name="p_sb", align_bytes=64)
+        t_sb = keep.tile([P, L], BF16, name="t_sb", align_bytes=64)
+        c_rows = keep.tile([P, P], BF16, name="c_rows", align_bytes=64)
+        c_sb = keep.tile([P, L // P], F32, name="c_sb", align_bytes=64)
+        pl_scales = keep.tile([P, QG, L], U8, name="pl_scales", align_bytes=64)
+        u_raw = [
+            keep.tile([P, n // P, D], BF16, name="u_raw_%d" % i, align_bytes=64)
+            for i, n in enumerate(CHUNKS)
+        ]
+
+        vs_view = vs_raw[:].bitcast(I32)
+        as_view = as_sb[:].bitcast(I32)
+        as_dst = as_view.rearrange("p (g n) -> p g n", g=GP)
+        as_src = a_scales.bitcast(I32)
+        vs_src = v_scales.bitcast(I32)
+        u_src = u.rearrange("(i p) k -> p i k", p=P)
+        t_bc = t.partition_broadcast(P)
+
+        nc.vector.memset(vs_view, 0)
+        nc.vector.memset(as_view, 0)
+        make_identity(nc, ident[:])
+        nc.gpsimd.memset(c_rows[:], 0.0)
+
+        def load_u(ci):
+            i0 = starts[ci] // P
+            nc.sync.dma_start(out=u_raw[ci][:], in_=u_src[:, i0 : i0 + CHUNKS[ci] // P, :])
+
+        def load_t(l0, l1):
+            nc.sync.dma_start(out=t_sb[:, l0:l1], in_=t_bc[:, l0:l1])
+
+        def load_v(g0, g1):
+            nc.sync.dma_start(
+                out=v_raw[:, 1024 * g0 : 1024 * g1].bitcast(I32),
+                in_=v_words[0, :, 1024 * g0 : 1024 * g1].bitcast(I32),
+            )
+
+        def load_a(g):
+            nc.sync.dma_start(out=a_sb[:, g, :].bitcast(I32), in_=a_words[g].bitcast(I32))
+
+        load_u(0)
+        load_v(0, 1)
+        for q in range(4):
+            nc.sync.dma_start(out=vs_view[32 * q : 32 * q + 4, :], in_=vs_src[0, 4 * q : 4 * q + 4, :])
+        nc.scalar.dma_start(out=b_sb[:], in_=b.rearrange("(g p t) -> p g t", g=GP, t=PACK))
+        load_t(0, CHUNKS[0])
+        nc.scalar.dma_start(out=p_sb[:], in_=p.rearrange("(g p t) -> p g t", g=GP, t=PACK))
+        load_v(1, GP)
+        load_u(1)
+        load_t(CHUNKS[0], L)
+        for q in range(4):
+            nc.sync.dma_start(
+                out=as_dst[32 * q : 32 * q + 4, :, :],
+                in_=as_src[:, 4 * q : 4 * q + 4, :].rearrange("g r n -> r g n"),
+            )
+        for g in range(GP):
+            load_a(g)
+        nc.sync.dma_start(out=c_rows[0 : L // P, :], in_=c.rearrange("(i p) -> i p", p=P))
+        for ci in range(2, len(CHUNKS)):
+            load_u(ci)
+
+        st = {}
+
+        def u_transposes(ci):
+            n = CHUNKS[ci] // P
+            words = u_raw[ci][:].rearrange("p i k -> p (i k)").bitcast(F32)
+            tr = psum.tile([P, n, 2, P], F32, name="utr", tag="tr", bufs=2)
+            for i in range(n):
+                for e in range(2):
+                    nc.tensor.transpose(tr[:, i, e, :], words[:, 256 * i + e : 256 * (i + 1) : 2], ident[:])
+            st["utr", ci] = tr
+
+        def u_copy(ci, vector):
+            n = CHUNKS[ci]
+            ug = work.tile([P, n * PACK], BF16, name="ug", tag="ug", bufs=2, align_bytes=64)
+            dst = ug[:].bitcast(F32).rearrange("p (i r e) -> p i r e", r=P, e=2)
+            src = st["utr", ci][:].rearrange("p i e r -> p i r e")
+            if vector:
+                nc.vector.tensor_copy(out=dst, in_=src)
+            else:
+                nc.scalar.copy(out=dst, in_=src)
+            st["ug", ci] = ug
+
+        def u_quant(ci):
+            n = CHUNKS[ci]
+            codes = work.tile([P, n], U32, name="uc", tag="uc", bufs=2, align_bytes=64)
+            scales = work.tile([P, n], U8, name="us", tag="us", bufs=2, align_bytes=64)
+            nc.vector.quantize_mx(out=codes[:].bitcast(E4X4), scales=scales[:], in_=st["ug", ci][:])
+            st["uq", ci] = (codes, scales)
+
+        def v_permute(g):
+            nc.vector.tensor_copy(
+                out=v_perm[:, g, :, :].rearrange("p t (m b) -> p t m b", b=2),
+                in_=v_raw[:, 1024 * g : 1024 * (g + 1)].rearrange("p (m t b) -> p t m b", t=PACK, b=2),
+            )
+
+        def vs_permute(g):
+            nc.vector.tensor_copy(
+                out=vs_perm[:, g, :, :],
+                in_=vs_raw[:, 512 * g : 512 * (g + 1)].rearrange("p (m t) -> p t m", t=PACK),
+            )
+
+        def mm1(k):
+            ci, g = units[k]
+            n = CHUNKS[ci]
+            codes, scales = st["uq", ci]
+            s1 = psum.tile([P, PACK, n], F32, name="s1", tag="s1", bufs=2)
+            for j in range(PACK):
+                nc.tensor.matmul_mx(
+                    out=s1[:, j, :],
+                    lhsT=v_perm[:, g, j, :].bitcast(E2X4),
+                    lhsT_scale=vs_perm[:, g, j, :],
+                    rhs=codes[:].bitcast(E4X4),
+                    rhs_scale=scales[:],
+                    start=True,
+                    stop=True,
+                )
+            st["s1", k] = s1
+
+        def z_step(k):
+            ci, g = units[k]
+            n, l0 = CHUNKS[ci], starts[ci]
+            z = work.tile([P, PACK, n], F32, name="z", tag="z", bufs=3, align_bytes=64)
+            for j in range(PACK):
+                nc.vector.scalar_tensor_tensor(
+                    out=z[:, j, :],
+                    in0=st["s1", k][:, j, :],
+                    scalar=b_sb[:, g, j : j + 1],
+                    in1=t_sb[:, l0 : l0 + n],
+                    op0=ADD,
+                    op1=MULT,
+                )
+            st["z", k] = z
+
+        def e_step(k):
+            n = CHUNKS[units[k][0]]
+            x = work.tile([P, n * PACK], F32, name="x", tag="x", bufs=3, align_bytes=64)
+            nc.scalar.activation(
+                out=x[:].rearrange("p (c i t) -> p c t i", i=4, t=PACK),
+                in_=st["z", k][:].rearrange("p t (c i) -> p c t i", i=4),
+                func=EXP,
+                scale=0.4,
+            )
+            st["x", k] = x
+
+        def m_step(k):
+            ci, g = units[k]
+            n = CHUNKS[ci]
+            m = work.tile([P, n * PACK], BF16, name="m", tag="m", bufs=3, align_bytes=64)
+            nc.vector.scalar_tensor_tensor(
+                out=m[:].rearrange("p (n t) -> p n t", t=PACK),
+                in0=st["x", k][:].rearrange("p (n t) -> p n t", t=PACK),
+                scalar=-1.0,
+                in1=p_sb[:, g, :].unsqueeze(1).to_broadcast([P, n, PACK]),
+                op0=ADD,
+                op1=MULT,
+            )
+            st["m", k] = m
+
+        def q_step(k):
+            ci, g = units[k]
+            n = CHUNKS[ci]
+            if g == 0:
+                mc = work.tile([P, GP, n], U32, name="mc", tag="mc", bufs=2, align_bytes=64)
+                ms = work.tile([P, GP, n], U8, name="ms", tag="ms", bufs=2, align_bytes=64)
+                st["mq", ci] = (mc, ms)
+            mc, ms = st["mq", ci]
+            nc.vector.quantize_mx(out=mc[:, g, :].bitcast(E4X4), scales=ms[:, g, :], in_=st["m", k][:])
+
+        def mm2(ci, j):
+            mc, ms = st["mq", ci]
+            cols = slice(P * j, P * (j + 1))
+            for h in range(QG):
+                acc = psum.tile([P, 512], F32, name="acc", tag="acc", bufs=2)
+                for g in range(GP):
+                    nc.tensor.matmul_mx(
+                        out=acc[:],
+                        lhsT=mc[:, g, cols].bitcast(E4X4),
+                        lhsT_scale=ms[:, g, cols],
+                        rhs=a_sb[:, g, 1024 * h : 1024 * (h + 1)].bitcast(E2X4),
+                        rhs_scale=as_sb[:, Q * g + 512 * h : Q * g + 512 * (h + 1)],
+                        start=(g == 0),
+                        stop=(g == GP - 1),
+                    )
+                st["acc", ci, j, h] = acc
+
+        def r_step(ci, j):
+            i = starts[ci] // P + j
+            r = work.tile([P, Q], F32, name="r", tag="r", bufs=3, align_bytes=64)
+            rb = work.tile([P, Q], BF16, name="rb", tag="rb", bufs=3, align_bytes=64)
+            on_scalar = i % 2 == 1
+            for h in range(QG):
+                acc = st["acc", ci, j, h]
+                nc.scalar.activation(
+                    out=r[:, 512 * h : 512 * (h + 1)], in_=acc[:], func=IDENT, bias=c_sb[:, i : i + 1]
+                )
+                if on_scalar:
+                    nc.scalar.activation(
+                        out=rb[:, 512 * h : 512 * (h + 1)], in_=acc[:], func=IDENT, bias=c_sb[:, i : i + 1]
+                    )
+            nc.sync.dma_start(out=out_0[P * i : P * (i + 1), :], in_=r[:])
+            st["r", ci, j] = (r, rb, on_scalar)
+
+        def round_step(ci, j):
+            r, rb, on_scalar = st["r", ci, j]
+            if not on_scalar:
+                nc.vector.tensor_copy(out=rb[:], in_=r[:])
+
+        def o_transposes(ci, j):
+            words = st["r", ci, j][1][:].bitcast(F32)
+            tr = psum.tile([P, QG, 2, P], F32, name="otr", tag="tr", bufs=2)
+            for g in range(QG):
+                for e in range(2):
+                    nc.tensor.transpose(tr[:, g, e, :], words[:, 256 * g + e : 256 * (g + 1) : 2], ident[:])
+            st["otr", ci, j] = tr
+
+        def o_copy(ci, j):
+            n = CHUNKS[ci]
+            if j == 0:
+                pb = work.tile([P, QG, n * PACK], BF16, name="pb", tag="pb", bufs=2, align_bytes=64)
+                st["pb", ci] = pb
+            pb = st["pb", ci]
+            dst = pb[:].rearrange("p g x -> p (g x)").bitcast(F32).rearrange(
+                "p (g r e) -> p g r e", g=QG, e=2
+            )
+            nc.scalar.copy(
+                out=dst[:, :, P * j : P * (j + 1), :],
+                in_=st["otr", ci, j][:].rearrange("p g e r -> p g r e"),
+            )
+
+        out_1_v = out_1.rearrange("g p l t -> p g (l t)").bitcast(I32)
+        out_2_v = out_2.bitcast(I32)
+        pls_v = pl_scales[:].rearrange("p g l -> p (g l)").bitcast(I32).rearrange("p (g l) -> p g l", g=QG)
+
+        def planes(ci):
+            n, l0 = CHUNKS[ci], starts[ci]
+            pc = work.tile([P, QG * n], U32, name="pc", tag="pc", bufs=2, align_bytes=64)
+            for g in range(QG):
+                nc.vector.quantize_mx(
+                    out=pc[:, g * n : (g + 1) * n].bitcast(E4X4),
+                    scales=pl_scales[:, g, l0 : l0 + n],
+                    in_=st["pb", ci][:, g, :],
+                )
+            nc.sync.dma_start(
+                out=out_1_v[:, :, l0 : l0 + n],
+                in_=pc[:].bitcast(I32).rearrange("p (g n) -> p g n", g=QG),
+            )
+
+        def store_scales(l0, l1):
+            for q in range(4):
+                nc.sync.dma_start(
+                    out=out_2_v[:, 4 * q : 4 * q + 4, l0 // 4 : l1 // 4].rearrange("g r l -> r g l"),
+                    in_=pls_v[32 * q : 32 * q + 4, :, l0 // 4 : l1 // 4],
+                )
+
+        u_transposes(0)
+        u_copy(0, True)
+        v_permute(0)
+        vs_permute(0)
+        u_quant(0)
+        mm1(0)
+        v_permute(1)
+        vs_permute(1)
+
+        def c_columns():
+            nc.vector.tensor_copy(out=ident_bf[:], in_=ident[:])
+            ctr = psum.tile([P, P], BF16, name="ctr", tag="tr", bufs=2)
+            nc.tensor.transpose(ctr[:], c_rows[:], ident_bf[:])
+            nc.vector.tensor_copy(out=c_sb[:], in_=ctr[:, 0 : L // P])
+
+        n_units = len(units)
+        last_of = {ci: GP * ci + GP - 1 for ci in range(len(CHUNKS))}
+        for k in range(n_units + 8):
+            if k == 3:
+                c_columns()
+            if k + 1 < n_units:
+                mm1(k + 1)
+            if k < n_units and units[k][1] == 0 and units[k][0] + 1 < len(CHUNKS):
+                u_transposes(units[k][0] + 1)
+            if 0 <= k - 1 < n_units:
+                e_step(k - 1)
+            for ci in range(len(CHUNKS)):
+                for j in range(CHUNKS[ci] // P):
+                    if k == last_of[ci] + 3 + j:
+                        r_step(ci, j)
+                    if k == last_of[ci] + 4 + j:
+                        o_copy(ci, j)
+            if k < n_units and units[k][1] == 0 and units[k][0] + 1 < len(CHUNKS):
+                u_copy(units[k][0] + 1, False)
+            if 0 <= k - 2 < n_units:
+                m_step(k - 2)
+            if k < n_units:
+                z_step(k)
+            if k == 0:
+                v_permute(2)
+                vs_permute(2)
+            if 0 <= k - 2 < n_units:
+                q_step(k - 2)
+            if k < n_units and units[k][1] == 1 and units[k][0] + 1 < len(CHUNKS):
+                u_quant(units[k][0] + 1)
+            for ci in range(len(CHUNKS)):
+                nt = CHUNKS[ci] // P
+                for j in range(nt):
+                    if k == last_of[ci] + 3 + j:
+                        round_step(ci, j)
+                if k == last_of[ci] + 4 + nt - 1:
+                    planes(ci)
+                    if ci == len(CHUNKS) - 2:
+                        store_scales(0, starts[-1])
+                    if ci == len(CHUNKS) - 1:
+                        store_scales(starts[-1], L)
+            for ci in range(len(CHUNKS)):
+                for j in range(CHUNKS[ci] // P):
+                    if k == last_of[ci] + 2 + j:
+                        mm2(ci, j)
+                    if k == last_of[ci] + 3 + j:
+                        o_transposes(ci, j)

@@ -22,7 +22,7 @@ P = 128
 PACK = 4
 GP = G // 512
 QG = Q // 512
-CHUNKS = (128, 256, 256, 256, 128)
+CHUNKS = (256, 256, 256, 256)
 
 
 def tile_knockoutpopulationgrowthguidereadout_x2_kernel(
@@ -36,7 +36,6 @@ def tile_knockoutpopulationgrowthguidereadout_x2_kernel(
         keep = ctx.enter_context(tc.tile_pool(name="keep", bufs=1))
         work = ctx.enter_context(tc.tile_pool(name="work", bufs=3))
         psum = ctx.enter_context(tc.psum_pool(name="psum", bufs=2))
-        ctx.enter_context(tc.manual_schedule())
 
         ident = keep.tile([P, P], F32, name="ident", align_bytes=64)
         ident_bf = keep.tile([P, P], BF16, name="ident_bf", align_bytes=64)
@@ -46,10 +45,11 @@ def tile_knockoutpopulationgrowthguidereadout_x2_kernel(
         vs_perm = keep.tile([P, GP, PACK, P], U8, name="vs_perm", align_bytes=64)
         a_sb = keep.tile([P, GP, 2 * Q], U8, name="a_sb", align_bytes=64)
         as_sb = keep.tile([P, GP * Q], U8, name="as_sb", align_bytes=64)
-        b_sb = keep.tile([P, GP, PACK], BF16, name="b_sb", align_bytes=64)
-        p_sb = keep.tile([P, GP, PACK], BF16, name="p_sb", align_bytes=64)
+        b_sb = keep.tile([P, GP, PACK], F32, name="b_sb", align_bytes=64)
+        p_sb = keep.tile([P, GP, PACK], F32, name="p_sb", align_bytes=64)
         t_sb = keep.tile([P, L], BF16, name="t_sb", align_bytes=64)
-        c_rows = keep.tile([P, P], BF16, name="c_rows", align_bytes=64)
+        rows = keep.tile([P, 512], BF16, name="rows", align_bytes=64)
+        t_cols = keep.tile([P, L // P], BF16, name="t_cols", align_bytes=64)
         c_sb = keep.tile([P, L // P], F32, name="c_sb", align_bytes=64)
         pl_scales = keep.tile([P, QG, L], U8, name="pl_scales", align_bytes=64)
         u_raw = [
@@ -63,19 +63,15 @@ def tile_knockoutpopulationgrowthguidereadout_x2_kernel(
         as_src = a_scales.bitcast(I32)
         vs_src = v_scales.bitcast(I32)
         u_src = u.rearrange("(i p) k -> p i k", p=P)
-        t_bc = t.partition_broadcast(P)
 
+        nc.vector.memset(rows[:], 0.0)
         nc.vector.memset(vs_view, 0)
-        nc.vector.memset(as_view, 0)
         make_identity(nc, ident[:])
-        nc.gpsimd.memset(c_rows[:], 0.0)
+        nc.gpsimd.memset(as_view, 0)
 
         def load_u(ci):
             i0 = starts[ci] // P
             nc.sync.dma_start(out=u_raw[ci][:], in_=u_src[:, i0 : i0 + CHUNKS[ci] // P, :])
-
-        def load_t(l0, l1):
-            nc.sync.dma_start(out=t_sb[:, l0:l1], in_=t_bc[:, l0:l1])
 
         def load_v(g0, g1):
             nc.sync.dma_start(
@@ -87,15 +83,15 @@ def tile_knockoutpopulationgrowthguidereadout_x2_kernel(
             nc.sync.dma_start(out=a_sb[:, g, :].bitcast(I32), in_=a_words[g].bitcast(I32))
 
         load_u(0)
+        nc.scalar.dma_start(out=rows[0:3, :], in_=b.rearrange("(g x) -> g x", g=GP))
+        nc.scalar.dma_start(out=rows[6:14, 0:P], in_=t.rearrange("(i x) -> i x", x=P))
         load_v(0, 1)
         for q in range(4):
             nc.sync.dma_start(out=vs_view[32 * q : 32 * q + 4, :], in_=vs_src[0, 4 * q : 4 * q + 4, :])
-        nc.scalar.dma_start(out=b_sb[:], in_=b.rearrange("(g p t) -> p g t", g=GP, t=PACK))
-        load_t(0, CHUNKS[0])
-        nc.scalar.dma_start(out=p_sb[:], in_=p.rearrange("(g p t) -> p g t", g=GP, t=PACK))
+        nc.scalar.dma_start(out=rows[3:6, :], in_=p.rearrange("(g x) -> g x", g=GP))
+        nc.scalar.dma_start(out=rows[14:22, 0:P], in_=c.rearrange("(i x) -> i x", x=P))
         load_v(1, GP)
         load_u(1)
-        load_t(CHUNKS[0], L)
         for q in range(4):
             nc.sync.dma_start(
                 out=as_dst[32 * q : 32 * q + 4, :, :],
@@ -103,7 +99,6 @@ def tile_knockoutpopulationgrowthguidereadout_x2_kernel(
             )
         for g in range(GP):
             load_a(g)
-        nc.sync.dma_start(out=c_rows[0 : L // P, :], in_=c.rearrange("(i p) -> i p", p=P))
         for ci in range(2, len(CHUNKS)):
             load_u(ci)
 
@@ -152,10 +147,13 @@ def tile_knockoutpopulationgrowthguidereadout_x2_kernel(
             ci, g = units[k]
             n = CHUNKS[ci]
             codes, scales = st["uq", ci]
-            s1 = psum.tile([P, PACK, n], F32, name="s1", tag="s1", bufs=2)
+            per = 512 // n
             for j in range(PACK):
+                if j % per == 0:
+                    s1 = psum.tile([P, per, n], F32, name="s1", tag="s1", bufs=4)
+                st["s1", k, j] = s1[:, j % per, :]
                 nc.tensor.matmul_mx(
-                    out=s1[:, j, :],
+                    out=st["s1", k, j],
                     lhsT=v_perm[:, g, j, :].bitcast(E2X4),
                     lhsT_scale=vs_perm[:, g, j, :],
                     rhs=codes[:].bitcast(E4X4),
@@ -163,7 +161,6 @@ def tile_knockoutpopulationgrowthguidereadout_x2_kernel(
                     start=True,
                     stop=True,
                 )
-            st["s1", k] = s1
 
         def z_step(k):
             ci, g = units[k]
@@ -172,7 +169,7 @@ def tile_knockoutpopulationgrowthguidereadout_x2_kernel(
             for j in range(PACK):
                 nc.vector.scalar_tensor_tensor(
                     out=z[:, j, :],
-                    in0=st["s1", k][:, j, :],
+                    in0=st["s1", k, j],
                     scalar=b_sb[:, g, j : j + 1],
                     in1=t_sb[:, l0 : l0 + n],
                     op0=ADD,
@@ -301,26 +298,40 @@ def tile_knockoutpopulationgrowthguidereadout_x2_kernel(
                     in_=pls_v[32 * q : 32 * q + 4, :, l0 // 4 : l1 // 4],
                 )
 
+        def t_spread(l0, l1, scalar):
+            tb = psum.tile([P, l1 - l0], BF16, name="tb", tag="acc", bufs=2)
+            for i in range(l0 // P, l1 // P):
+                nc.tensor.transpose(
+                    tb[:, P * i - l0 : P * (i + 1) - l0], t_cols[:, i : i + 1].to_broadcast([P, P]), ident_bf[:]
+                )
+            if scalar:
+                nc.scalar.copy(out=t_sb[:, l0:l1], in_=tb[:])
+            else:
+                nc.vector.tensor_copy(out=t_sb[:, l0:l1], in_=tb[:])
+
+        nc.vector.tensor_copy(out=ident_bf[:], in_=ident[:])
         u_transposes(0)
         u_copy(0, True)
+        vec = psum.tile([P, PACK + 1, P], BF16, name="vec", tag="acc", bufs=2)
+        nc.tensor.transpose(vec[:, PACK, :], rows[:, 0:P], ident_bf[:])
+        for j in range(PACK):
+            nc.tensor.transpose(vec[:, j, :], rows[:, j : 512 : PACK], ident_bf[:])
         v_permute(0)
-        vs_permute(0)
+        nc.vector.tensor_copy(out=t_cols[:], in_=vec[:, PACK, 6:14])
         u_quant(0)
+        vs_permute(0)
         mm1(0)
+        nc.vector.tensor_copy(out=b_sb[:], in_=vec[:, 0:PACK, 0:3].rearrange("p t g -> p g t"))
+        nc.vector.tensor_copy(out=p_sb[:], in_=vec[:, 0:PACK, 3:6].rearrange("p t g -> p g t"))
+        nc.vector.tensor_copy(out=c_sb[:], in_=vec[:, PACK, 14:22])
+        t_spread(0, CHUNKS[0], False)
         v_permute(1)
         vs_permute(1)
 
-        def c_columns():
-            nc.vector.tensor_copy(out=ident_bf[:], in_=ident[:])
-            ctr = psum.tile([P, P], BF16, name="ctr", tag="tr", bufs=2)
-            nc.tensor.transpose(ctr[:], c_rows[:], ident_bf[:])
-            nc.vector.tensor_copy(out=c_sb[:], in_=ctr[:, 0 : L // P])
 
         n_units = len(units)
         last_of = {ci: GP * ci + GP - 1 for ci in range(len(CHUNKS))}
         for k in range(n_units + 8):
-            if k == 3:
-                c_columns()
             if k + 1 < n_units:
                 mm1(k + 1)
             if k < n_units and units[k][1] == 0 and units[k][0] + 1 < len(CHUNKS):
@@ -333,8 +344,10 @@ def tile_knockoutpopulationgrowthguidereadout_x2_kernel(
                         r_step(ci, j)
                     if k == last_of[ci] + 4 + j:
                         o_copy(ci, j)
-            if k < n_units and units[k][1] == 0 and units[k][0] + 1 < len(CHUNKS):
+            if k < n_units and units[k][1] == 1 and units[k][0] + 1 < len(CHUNKS):
                 u_copy(units[k][0] + 1, False)
+            if k == 1:
+                t_spread(CHUNKS[0], L, True)
             if 0 <= k - 2 < n_units:
                 m_step(k - 2)
             if k < n_units:

@@ -23,6 +23,8 @@ PACK = 4
 GP = G // 512
 QG = Q // 512
 CHUNKS = (256, 256, 256, 256)
+KIND = "GGGGGGDD"
+ASSIST = ()
 
 
 def tile_knockoutpopulationgrowthguidereadout_x2_kernel(
@@ -36,6 +38,7 @@ def tile_knockoutpopulationgrowthguidereadout_x2_kernel(
         keep = ctx.enter_context(tc.tile_pool(name="keep", bufs=1))
         work = ctx.enter_context(tc.tile_pool(name="work", bufs=3))
         psum = ctx.enter_context(tc.psum_pool(name="psum", bufs=2))
+        ctx.enter_context(tc.manual_schedule())
 
         ident = keep.tile([P, P], F32, name="ident", align_bytes=64)
         ident_bf = keep.tile([P, P], BF16, name="ident_bf", align_bytes=64)
@@ -45,12 +48,13 @@ def tile_knockoutpopulationgrowthguidereadout_x2_kernel(
         vs_perm = keep.tile([P, GP, PACK, P], U8, name="vs_perm", align_bytes=64)
         a_sb = keep.tile([P, GP, 2 * Q], U8, name="a_sb", align_bytes=64)
         as_sb = keep.tile([P, GP * Q], U8, name="as_sb", align_bytes=64)
-        b_sb = keep.tile([P, GP, PACK], F32, name="b_sb", align_bytes=64)
-        p_sb = keep.tile([P, GP, PACK], F32, name="p_sb", align_bytes=64)
+        cols_bt = keep.tile([P, PACK + 1, 16], BF16, name="cols_bt", align_bytes=64)
+        cols_pc = keep.tile([P, PACK + 1, 16], F32, name="cols_pc", align_bytes=64)
+        minus_p = keep.tile([P, PACK, GP], F32, name="minus_p", align_bytes=64)
+        p_sb = keep.tile([P, GP, PACK], BF16, name="p_sb", align_bytes=64)
         t_sb = keep.tile([P, L], BF16, name="t_sb", align_bytes=64)
-        rows = keep.tile([P, 512], BF16, name="rows", align_bytes=64)
-        t_cols = keep.tile([P, L // P], BF16, name="t_cols", align_bytes=64)
-        c_sb = keep.tile([P, L // P], F32, name="c_sb", align_bytes=64)
+        rows_bt = keep.tile([P, 512], BF16, name="rows_bt", align_bytes=64)
+        rows_pc = keep.tile([P, 512], BF16, name="rows_pc", align_bytes=64)
         pl_scales = keep.tile([P, QG, L], U8, name="pl_scales", align_bytes=64)
         u_raw = [
             keep.tile([P, n // P, D], BF16, name="u_raw_%d" % i, align_bytes=64)
@@ -64,10 +68,11 @@ def tile_knockoutpopulationgrowthguidereadout_x2_kernel(
         vs_src = v_scales.bitcast(I32)
         u_src = u.rearrange("(i p) k -> p i k", p=P)
 
-        nc.vector.memset(rows[:], 0.0)
+        nc.vector.memset(rows_bt[:], 0.0)
         nc.vector.memset(vs_view, 0)
+        nc.gpsimd.memset(rows_pc[:], 0.0)
         make_identity(nc, ident[:])
-        nc.gpsimd.memset(as_view, 0)
+        nc.vector.memset(as_view, 0)
 
         def load_u(ci):
             i0 = starts[ci] // P
@@ -83,14 +88,13 @@ def tile_knockoutpopulationgrowthguidereadout_x2_kernel(
             nc.sync.dma_start(out=a_sb[:, g, :].bitcast(I32), in_=a_words[g].bitcast(I32))
 
         load_u(0)
-        nc.scalar.dma_start(out=rows[0:3, :], in_=b.rearrange("(g x) -> g x", g=GP))
-        nc.scalar.dma_start(out=rows[6:14, 0:P], in_=t.rearrange("(i x) -> i x", x=P))
-        load_v(0, 1)
+        nc.scalar.dma_start(out=rows_bt[0:3, :], in_=b.rearrange("(g x) -> g x", g=GP))
+        nc.scalar.dma_start(out=rows_bt[3:11, 0:P], in_=t.rearrange("(i x) -> i x", x=P))
+        nc.gpsimd.dma_start(out=rows_pc[0:3, :], in_=p.rearrange("(g x) -> g x", g=GP))
+        nc.gpsimd.dma_start(out=rows_pc[3:11, 0:P], in_=c.rearrange("(i x) -> i x", x=P))
+        load_v(0, GP)
         for q in range(4):
             nc.sync.dma_start(out=vs_view[32 * q : 32 * q + 4, :], in_=vs_src[0, 4 * q : 4 * q + 4, :])
-        nc.scalar.dma_start(out=rows[3:6, :], in_=p.rearrange("(g x) -> g x", g=GP))
-        nc.scalar.dma_start(out=rows[14:22, 0:P], in_=c.rearrange("(i x) -> i x", x=P))
-        load_v(1, GP)
         load_u(1)
         for q in range(4):
             nc.sync.dma_start(
@@ -170,7 +174,7 @@ def tile_knockoutpopulationgrowthguidereadout_x2_kernel(
                 nc.vector.scalar_tensor_tensor(
                     out=z[:, j, :],
                     in0=st["s1", k, j],
-                    scalar=b_sb[:, g, j : j + 1],
+                    scalar=cols_bt[:, j, g : g + 1],
                     in1=t_sb[:, l0 : l0 + n],
                     op0=ADD,
                     op1=MULT,
@@ -178,20 +182,56 @@ def tile_knockoutpopulationgrowthguidereadout_x2_kernel(
             st["z", k] = z
 
         def e_step(k):
-            n = CHUNKS[units[k][0]]
+            ci, g = units[k]
+            n = CHUNKS[ci]
+            if k in ASSIST:
+                x = work.tile([P, PACK, n], F32, name="xs", tag="x", bufs=3, align_bytes=64)
+                nc.scalar.activation(out=x[:], in_=st["z", k][:], func=EXP, scale=0.4)
+                y = work.tile([P, PACK, n], BF16, name="y", tag="y", bufs=2, align_bytes=64)
+                for j in range(PACK):
+                    nc.scalar.activation(
+                        out=y[:, j, :],
+                        in_=x[:, j, :],
+                        func=IDENT,
+                        scale=cols_pc[:, j, g : g + 1],
+                        bias=minus_p[:, j, g : g + 1],
+                    )
+                st["x", k] = y
+                return
             x = work.tile([P, n * PACK], F32, name="x", tag="x", bufs=3, align_bytes=64)
-            nc.scalar.activation(
-                out=x[:].rearrange("p (c i t) -> p c t i", i=4, t=PACK),
-                in_=st["z", k][:].rearrange("p t (c i) -> p c t i", i=4),
-                func=EXP,
-                scale=0.4,
-            )
+            step = P if k == len(units) - 1 else n
+            for l in range(0, n, step):
+                nc.scalar.activation(
+                    out=x[:, PACK * l : PACK * (l + step)].rearrange("p (c i t) -> p c t i", i=4, t=PACK),
+                    in_=st["z", k][:, :, l : l + step].rearrange("p t (c i) -> p c t i", i=4),
+                    func=EXP,
+                    scale=0.4,
+                )
             st["x", k] = x
 
         def m_step(k):
             ci, g = units[k]
             n = CHUNKS[ci]
             m = work.tile([P, n * PACK], BF16, name="m", tag="m", bufs=3, align_bytes=64)
+            st["m", k] = m
+            if k == len(units) - 1:
+                for i in range(n // P):
+                    part = slice(512 * i, 512 * (i + 1))
+                    nc.vector.scalar_tensor_tensor(
+                        out=m[:, part].rearrange("p (n t) -> p n t", t=PACK),
+                        in0=st["x", k][:, part].rearrange("p (n t) -> p n t", t=PACK),
+                        scalar=-1.0,
+                        in1=p_sb[:, g, :].unsqueeze(1).to_broadcast([P, P, PACK]),
+                        op0=ADD,
+                        op1=MULT,
+                    )
+                return
+            if k in ASSIST:
+                nc.vector.tensor_copy(
+                    out=m[:].rearrange("p (c i t) -> p c t i", i=4, t=PACK),
+                    in_=st["x", k][:].rearrange("p t (c i) -> p c t i", i=4),
+                )
+                return
             nc.vector.scalar_tensor_tensor(
                 out=m[:].rearrange("p (n t) -> p n t", t=PACK),
                 in0=st["x", k][:].rearrange("p (n t) -> p n t", t=PACK),
@@ -200,7 +240,6 @@ def tile_knockoutpopulationgrowthguidereadout_x2_kernel(
                 op0=ADD,
                 op1=MULT,
             )
-            st["m", k] = m
 
         def q_step(k):
             ci, g = units[k]
@@ -210,14 +249,22 @@ def tile_knockoutpopulationgrowthguidereadout_x2_kernel(
                 ms = work.tile([P, GP, n], U8, name="ms", tag="ms", bufs=2, align_bytes=64)
                 st["mq", ci] = (mc, ms)
             mc, ms = st["mq", ci]
-            nc.vector.quantize_mx(out=mc[:, g, :].bitcast(E4X4), scales=ms[:, g, :], in_=st["m", k][:])
+            step = P if k == len(units) - 1 else n
+            for l in range(0, n, step):
+                part = slice(l, l + step)
+                nc.vector.quantize_mx(
+                    out=mc[:, g, part].bitcast(E4X4), scales=ms[:, g, part], in_=st["m", k][:, PACK * l : PACK * (l + step)]
+                )
 
-        def mm2(ci, j):
+        def mm2(ci, j, passes=range(GP), tag="acc", bufs=2):
             mc, ms = st["mq", ci]
             cols = slice(P * j, P * (j + 1))
             for h in range(QG):
-                acc = psum.tile([P, 512], F32, name="acc", tag="acc", bufs=2)
-                for g in range(GP):
+                if 0 in passes:
+                    acc = psum.tile([P, 512], F32, name="acc", tag=tag, bufs=bufs)
+                    st["acc", ci, j, h] = acc
+                acc = st["acc", ci, j, h]
+                for g in passes:
                     nc.tensor.matmul_mx(
                         out=acc[:],
                         lhsT=mc[:, g, cols].bitcast(E4X4),
@@ -227,32 +274,51 @@ def tile_knockoutpopulationgrowthguidereadout_x2_kernel(
                         start=(g == 0),
                         stop=(g == GP - 1),
                     )
-                st["acc", ci, j, h] = acc
 
         def r_step(ci, j):
             i = starts[ci] // P + j
             r = work.tile([P, Q], F32, name="r", tag="r", bufs=3, align_bytes=64)
             rb = work.tile([P, Q], BF16, name="rb", tag="rb", bufs=3, align_bytes=64)
-            on_scalar = i % 2 == 1
+            kind = KIND[i]
             for h in range(QG):
+                half = slice(512 * h, 512 * (h + 1))
                 acc = st["acc", ci, j, h]
-                nc.scalar.activation(
-                    out=r[:, 512 * h : 512 * (h + 1)], in_=acc[:], func=IDENT, bias=c_sb[:, i : i + 1]
-                )
-                if on_scalar:
+                if kind == "D" and h == 1:
+                    nc.vector.tensor_scalar(
+                        out=r[:, half], in0=acc[:], scalar1=cols_pc[:, PACK, 3 + i : 4 + i], scalar2=None, op0=ADD
+                    )
+                else:
                     nc.scalar.activation(
-                        out=rb[:, 512 * h : 512 * (h + 1)], in_=acc[:], func=IDENT, bias=c_sb[:, i : i + 1]
+                        out=r[:, half], in_=acc[:], func=IDENT, bias=cols_pc[:, PACK, 3 + i : 4 + i]
+                    )
+                if kind == "B":
+                    nc.scalar.activation(
+                        out=rb[:, half], in_=acc[:], func=IDENT, bias=cols_pc[:, PACK, 3 + i : 4 + i]
                     )
             nc.sync.dma_start(out=out_0[P * i : P * (i + 1), :], in_=r[:])
-            st["r", ci, j] = (r, rb, on_scalar)
+            st["r", ci, j] = (r, rb, kind)
 
         def round_step(ci, j):
-            r, rb, on_scalar = st["r", ci, j]
-            if not on_scalar:
-                nc.vector.tensor_copy(out=rb[:], in_=r[:])
+            r, rb, kind = st["r", ci, j]
+            for h in range(QG):
+                half = slice(512 * h, 512 * (h + 1))
+                if kind == "G":
+                    nc.gpsimd.tensor_scalar(
+                        out=rb[:, half], in0=r[:, half], scalar1=1.0, scalar2=0.0, op0=MULT, op1=ADD
+                    )
+                elif kind in "AD":
+                    nc.vector.tensor_copy(out=rb[:, half], in_=r[:, half])
 
         def o_transposes(ci, j):
-            words = st["r", ci, j][1][:].bitcast(F32)
+            r, rb, kind = st["r", ci, j]
+            if kind == "C":
+                for g in range(QG):
+                    tr = psum.tile([P, PACK, P], F32, name="otr", tag="tr", bufs=2)
+                    for e in range(PACK):
+                        nc.tensor.transpose(tr[:, e, :], r[:, 512 * g + e : 512 * (g + 1) : PACK], ident[:])
+                    st["otr", ci, j, g] = tr
+                return
+            words = rb[:].bitcast(F32)
             tr = psum.tile([P, QG, 2, P], F32, name="otr", tag="tr", bufs=2)
             for g in range(QG):
                 for e in range(2):
@@ -265,13 +331,23 @@ def tile_knockoutpopulationgrowthguidereadout_x2_kernel(
                 pb = work.tile([P, QG, n * PACK], BF16, name="pb", tag="pb", bufs=2, align_bytes=64)
                 st["pb", ci] = pb
             pb = st["pb", ci]
+            if st["r", ci, j][2] == "C":
+                for g in range(QG):
+                    nc.scalar.copy(
+                        out=pb[:, g, 512 * j : 512 * (j + 1)].rearrange("p (r t) -> p r t", t=PACK),
+                        in_=st["otr", ci, j, g][:].rearrange("p t r -> p r t"),
+                    )
+                return
             dst = pb[:].rearrange("p g x -> p (g x)").bitcast(F32).rearrange(
                 "p (g r e) -> p g r e", g=QG, e=2
             )
-            nc.scalar.copy(
-                out=dst[:, :, P * j : P * (j + 1), :],
-                in_=st["otr", ci, j][:].rearrange("p g e r -> p g r e"),
-            )
+            src = st["otr", ci, j][:].rearrange("p g e r -> p g r e")
+            here = slice(P * j, P * (j + 1))
+            if st["r", ci, j][2] == "D":
+                nc.scalar.copy(out=dst[:, 0, here, :], in_=src[:, 0])
+                nc.vector.tensor_copy(out=dst[:, 1, here, :], in_=src[:, 1])
+            else:
+                nc.scalar.copy(out=dst[:, :, here, :], in_=src)
 
         out_1_v = out_1.rearrange("g p l t -> p g (l t)").bitcast(I32)
         out_2_v = out_2.bitcast(I32)
@@ -302,52 +378,59 @@ def tile_knockoutpopulationgrowthguidereadout_x2_kernel(
             tb = psum.tile([P, l1 - l0], BF16, name="tb", tag="acc", bufs=2)
             for i in range(l0 // P, l1 // P):
                 nc.tensor.transpose(
-                    tb[:, P * i - l0 : P * (i + 1) - l0], t_cols[:, i : i + 1].to_broadcast([P, P]), ident_bf[:]
+                    tb[:, P * i - l0 : P * (i + 1) - l0], cols_bt[:, PACK, 3 + i : 4 + i].to_broadcast([P, P]), ident_bf[:]
                 )
             if scalar:
                 nc.scalar.copy(out=t_sb[:, l0:l1], in_=tb[:])
             else:
                 nc.vector.tensor_copy(out=t_sb[:, l0:l1], in_=tb[:])
 
+        def columns(rows):
+            vec = psum.tile([P, PACK + 1, P], BF16, name="vec", tag="acc", bufs=2)
+            for j in range(PACK):
+                nc.tensor.transpose(vec[:, j, :], rows[:, j : 512 : PACK], ident_bf[:])
+            nc.tensor.transpose(vec[:, PACK, :], rows[:, 0:P], ident_bf[:])
+            return vec
+
         nc.vector.tensor_copy(out=ident_bf[:], in_=ident[:])
         u_transposes(0)
-        u_copy(0, True)
-        vec = psum.tile([P, PACK + 1, P], BF16, name="vec", tag="acc", bufs=2)
-        nc.tensor.transpose(vec[:, PACK, :], rows[:, 0:P], ident_bf[:])
-        for j in range(PACK):
-            nc.tensor.transpose(vec[:, j, :], rows[:, j : 512 : PACK], ident_bf[:])
+        u_copy(0, False)
+        vec_bt = columns(rows_bt)
+        nc.scalar.copy(out=cols_bt[:, :, 0:11], in_=vec_bt[:, :, 0:11])
         v_permute(0)
-        nc.vector.tensor_copy(out=t_cols[:], in_=vec[:, PACK, 6:14])
-        u_quant(0)
         vs_permute(0)
+        u_quant(0)
+        t_spread(0, CHUNKS[0], True)
         mm1(0)
-        nc.vector.tensor_copy(out=b_sb[:], in_=vec[:, 0:PACK, 0:3].rearrange("p t g -> p g t"))
-        nc.vector.tensor_copy(out=p_sb[:], in_=vec[:, 0:PACK, 3:6].rearrange("p t g -> p g t"))
-        nc.vector.tensor_copy(out=c_sb[:], in_=vec[:, PACK, 14:22])
-        t_spread(0, CHUNKS[0], False)
         v_permute(1)
         vs_permute(1)
-
+        vec_pc = columns(rows_pc)
+        nc.scalar.copy(out=p_sb[:], in_=vec_pc[:, 0:PACK, 0:GP].rearrange("p t g -> p g t"))
+        nc.scalar.copy(out=cols_pc[:, :, 0:11], in_=vec_pc[:, :, 0:11])
+        nc.scalar.activation(out=minus_p[:], in_=vec_pc[:, 0:PACK, 0:GP], func=IDENT, scale=-1.0)
 
         n_units = len(units)
-        last_of = {ci: GP * ci + GP - 1 for ci in range(len(CHUNKS))}
-        for k in range(n_units + 8):
+        last = len(CHUNKS) - 1
+        for k in range(n_units + 2):
+            c1, g1 = divmod(k, GP)
+            done = (k - 5) // GP
+            taking_out = k >= 5 and done < last
             if k + 1 < n_units:
                 mm1(k + 1)
-            if k < n_units and units[k][1] == 0 and units[k][0] + 1 < len(CHUNKS):
-                u_transposes(units[k][0] + 1)
+            if g1 == 0 and c1 + 1 < len(CHUNKS):
+                u_transposes(c1 + 1)
+            if k == 0:
+                u_copy(1, False)
             if 0 <= k - 1 < n_units:
                 e_step(k - 1)
-            for ci in range(len(CHUNKS)):
-                for j in range(CHUNKS[ci] // P):
-                    if k == last_of[ci] + 3 + j:
-                        r_step(ci, j)
-                    if k == last_of[ci] + 4 + j:
-                        o_copy(ci, j)
-            if k < n_units and units[k][1] == 1 and units[k][0] + 1 < len(CHUNKS):
-                u_copy(units[k][0] + 1, False)
             if k == 1:
                 t_spread(CHUNKS[0], L, True)
+            if g1 == 1 and 0 < c1 and c1 + 1 < len(CHUNKS):
+                u_copy(c1 + 1, False)
+            if taking_out and g1 == 2:
+                r_step(done, 0)
+            if taking_out and g1 == 0:
+                r_step(done, 1)
             if 0 <= k - 2 < n_units:
                 m_step(k - 2)
             if k < n_units:
@@ -357,22 +440,36 @@ def tile_knockoutpopulationgrowthguidereadout_x2_kernel(
                 vs_permute(2)
             if 0 <= k - 2 < n_units:
                 q_step(k - 2)
-            if k < n_units and units[k][1] == 1 and units[k][0] + 1 < len(CHUNKS):
-                u_quant(units[k][0] + 1)
-            for ci in range(len(CHUNKS)):
-                nt = CHUNKS[ci] // P
-                for j in range(nt):
-                    if k == last_of[ci] + 3 + j:
-                        round_step(ci, j)
-                if k == last_of[ci] + 4 + nt - 1:
-                    planes(ci)
-                    if ci == len(CHUNKS) - 2:
-                        store_scales(0, starts[-1])
-                    if ci == len(CHUNKS) - 1:
-                        store_scales(starts[-1], L)
-            for ci in range(len(CHUNKS)):
-                for j in range(CHUNKS[ci] // P):
-                    if k == last_of[ci] + 2 + j:
-                        mm2(ci, j)
-                    if k == last_of[ci] + 3 + j:
-                        o_transposes(ci, j)
+            if g1 == 1 and c1 + 1 < len(CHUNKS):
+                u_quant(c1 + 1)
+            if taking_out and g1 == 2:
+                round_step(done, 0)
+            if taking_out and g1 == 0:
+                round_step(done, 1)
+            if g1 == 0 and k >= 9:
+                planes(k // GP - 3)
+            if taking_out and g1 == 0:
+                o_transposes(done, 0)
+                o_copy(done, 0)
+            if taking_out and g1 == 1:
+                o_transposes(done, 1)
+                o_copy(done, 1)
+            if k >= 4 and (k - 4) // GP < last and g1 > 0:
+                mm2((k - 4) // GP, g1 - 1)
+            if k == n_units:
+                for j in range(2):
+                    mm2(last, j, range(0, 2), "s1", 4)
+
+        store_scales(0, starts[-2])
+        for j in range(2):
+            mm2(last, j, range(2, 3))
+        for j in range(2):
+            r_step(last, j)
+            round_step(last, j)
+            o_transposes(last, j)
+        planes(last - 1)
+        store_scales(starts[-2], starts[-1])
+        for j in range(2):
+            o_copy(last, j)
+        planes(last)
+        store_scales(starts[-1], L)

@@ -23,8 +23,8 @@ PACK = 4
 GP = G // 512
 QG = Q // 512
 CHUNKS = (256, 256, 256, 256)
-KIND = "GGGGGGDD"
-ASSIST = ()
+KIND = "AABBAADD"
+ASSIST = (2,)
 
 
 def tile_knockoutpopulationgrowthguidereadout_x2_kernel(
@@ -419,11 +419,10 @@ def tile_knockoutpopulationgrowthguidereadout_x2_kernel(
                 mm1(k + 1)
             if g1 == 0 and c1 + 1 < len(CHUNKS):
                 u_transposes(c1 + 1)
-            if k == 0:
-                u_copy(1, False)
             if 0 <= k - 1 < n_units:
                 e_step(k - 1)
             if k == 1:
+                u_copy(1, False)
                 t_spread(CHUNKS[0], L, True)
             if g1 == 1 and 0 < c1 and c1 + 1 < len(CHUNKS):
                 u_copy(c1 + 1, False)

from contextlib import ExitStack

import concourse.mybir as mybir
from concourse.masks import make_identity

L, D, G, Q = 1024, 512, 1536, 1024
FLOPS = 2 * L * D * G + 2 * L * G * Q

F32 = mybir.dt.float32
BF16 = mybir.dt.bfloat16
U32 = mybir.dt.uint32
I32 = mybir.dt.int32
U8 = mybir.dt.uint8
E4X4 = mybir.dt.float8_e4m3fn_x4
E2X4 = mybir.dt.float4_e2m1fn_x4
ADD = mybir.AluOpType.add
MULT = mybir.AluOpType.mult
EXP = mybir.ActivationFunctionType.Exp
IDENT = mybir.ActivationFunctionType.Identity

P = 128
PACK = 4
GP = G // 512
QG = Q // 512
CHUNKS = (256, 256, 256, 256)
KIND = "AABBAADD"
ASSIST = (2,)


def tile_knockoutpopulationgrowthguidereadout_x2_kernel(
    tc, u, v_words, v_scales, b, t, p, a_words, a_scales, c, out_0, out_1, out_2
):
    nc = tc.nc
    starts = [sum(CHUNKS[:i]) for i in range(len(CHUNKS))]
    units = [(ci, g) for ci in range(len(CHUNKS)) for g in range(GP)]

    with ExitStack() as ctx:
        keep = ctx.enter_context(tc.tile_pool(name="keep", bufs=1))
        work = ctx.enter_context(tc.tile_pool(name="work", bufs=3))
        psum = ctx.enter_context(tc.psum_pool(name="psum", bufs=2))
        ctx.enter_context(tc.manual_schedule())

        ident = keep.tile([P, P], F32, name="ident", align_bytes=64)
        ident_bf = keep.tile([P, P], BF16, name="ident_bf", align_bytes=64)
        v_raw = keep.tile([P, 2 * G], U8, name="v_raw", align_bytes=64)
        vs_raw = keep.tile([P, G], U8, name="vs_raw", align_bytes=64)
        v_perm = keep.tile([P, GP, PACK, 2 * P], U8, name="v_perm", align_bytes=64)
        vs_perm = keep.tile([P, GP, PACK, P], U8, name="vs_perm", align_bytes=64)
        a_sb = keep.tile([P, GP, 2 * Q], U8, name="a_sb", align_bytes=64)
        as_sb = keep.tile([P, GP * Q], U8, name="as_sb", align_bytes=64)
        cols_bt = keep.tile([P, PACK + 1, 16], BF16, name="cols_bt", align_bytes=64)
        cols_pc = keep.tile([P, PACK + 1, 16], F32, name="cols_pc", align_bytes=64)
        minus_p = keep.tile([P, PACK, GP], F32, name="minus_p", align_bytes=64)
        p_sb = keep.tile([P, GP, PACK], BF16, name="p_sb", align_bytes=64)
        t_sb = keep.tile([P, L], BF16, name="t_sb", align_bytes=64)
        rows_bt = keep.tile([P, 512], BF16, name="rows_bt", align_bytes=64)
        rows_pc = keep.tile([P, 512], BF16, name="rows_pc", align_bytes=64)
        pl_scales = keep.tile([P, QG, L], U8, name="pl_scales", align_bytes=64)
        u_raw = [
            keep.tile([P, n // P, D], BF16, name="u_raw_%d" % i, align_bytes=64)
            for i, n in enumerate(CHUNKS)
        ]

        vs_view = vs_raw[:].bitcast(I32)
        as_view = as_sb[:].bitcast(I32)
        as_dst = as_view.rearrange("p (g n) -> p g n", g=GP)
        as_src = a_scales.bitcast(I32)
        vs_src = v_scales.bitcast(I32)
        u_src = u.rearrange("(i p) k -> p i k", p=P)

        nc.vector.memset(rows_bt[:], 0.0)
        nc.vector.memset(vs_view, 0)
        nc.gpsimd.memset(rows_pc[:], 0.0)
        make_identity(nc, ident[:])
        nc.vector.memset(as_view, 0)

        def load_u(ci):
            i0 = starts[ci] // P
            nc.sync.dma_start(out=u_raw[ci][:], in_=u_src[:, i0 : i0 + CHUNKS[ci] // P, :])

        def load_v(g0, g1):
            nc.sync.dma_start(
                out=v_raw[:, 1024 * g0 : 1024 * g1].bitcast(I32),
                in_=v_words[0, :, 1024 * g0 : 1024 * g1].bitcast(I32),
            )

        def load_a(g):
            nc.sync.dma_start(out=a_sb[:, g, :].bitcast(I32), in_=a_words[g].bitcast(I32))

        load_u(0)
        nc.scalar.dma_start(out=rows_bt[0:3, :], in_=b.rearrange("(g x) -> g x", g=GP))
        nc.scalar.dma_start(out=rows_bt[3:11, 0:P], in_=t.rearrange("(i x) -> i x", x=P))
        nc.gpsimd.dma_start(out=rows_pc[0:3, :], in_=p.rearrange("(g x) -> g x", g=GP))
        nc.gpsimd.dma_start(out=rows_pc[3:11, 0:P], in_=c.rearrange("(i x) -> i x", x=P))
        load_v(0, GP)
        for q in range(4):
            nc.sync.dma_start(out=vs_view[32 * q : 32 * q + 4, :], in_=vs_src[0, 4 * q : 4 * q + 4, :])
        load_u(1)
        for q in range(4):
            nc.sync.dma_start(
                out=as_dst[32 * q : 32 * q + 4, :, :],
                in_=as_src[:, 4 * q : 4 * q + 4, :].rearrange("g r n -> r g n"),
            )
        for g in range(GP):
            load_a(g)
        for ci in range(2, len(CHUNKS)):
            load_u(ci)

        st = {}

        def u_transposes(ci):
            n = CHUNKS[ci] // P
            words = u_raw[ci][:].rearrange("p i k -> p (i k)").bitcast(F32)
            tr = psum.tile([P, n, 2, P], F32, name="utr", tag="tr", bufs=2)
            for i in range(n):
                for e in range(2):
                    nc.tensor.transpose(tr[:, i, e, :], words[:, 256 * i + e : 256 * (i + 1) : 2], ident[:])
            st["utr", ci] = tr

        def u_copy(ci, vector):
            n = CHUNKS[ci]
            ug = work.tile([P, n * PACK], BF16, name="ug", tag="ug", bufs=2, align_bytes=64)
            dst = ug[:].bitcast(F32).rearrange("p (i r e) -> p i r e", r=P, e=2)
            src = st["utr", ci][:].rearrange("p i e r -> p i r e")
            if vector:
                nc.vector.tensor_copy(out=dst, in_=src)
            else:
                nc.scalar.copy(out=dst, in_=src)
            st["ug", ci] = ug

        def u_quant(ci):
            n = CHUNKS[ci]
            codes = work.tile([P, n], U32, name="uc", tag="uc", bufs=2, align_bytes=64)
            scales = work.tile([P, n], U8, name="us", tag="us", bufs=2, align_bytes=64)
            nc.vector.quantize_mx(out=codes[:].bitcast(E4X4), scales=scales[:], in_=st["ug", ci][:])
            st["uq", ci] = (codes, scales)

        def v_permute(g):
            nc.vector.tensor_copy(
                out=v_perm[:, g, :, :].rearrange("p t (m b) -> p t m b", b=2),
                in_=v_raw[:, 1024 * g : 1024 * (g + 1)].rearrange("p (m t b) -> p t m b", t=PACK, b=2),
            )

        def vs_permute(g):
            nc.vector.tensor_copy(
                out=vs_perm[:, g, :, :],
                in_=vs_raw[:, 512 * g : 512 * (g + 1)].rearrange("p (m t) -> p t m", t=PACK),
            )

        def mm1(k):
            ci, g = units[k]
            n = CHUNKS[ci]
            codes, scales = st["uq", ci]
            per = 512 // n
            for j in range(PACK):
                if j % per == 0:
                    s1 = psum.tile([P, per, n], F32, name="s1", tag="s1", bufs=4)
                st["s1", k, j] = s1[:, j % per, :]
                nc.tensor.matmul_mx(
                    out=st["s1", k, j],
                    lhsT=v_perm[:, g, j, :].bitcast(E2X4),
                    lhsT_scale=vs_perm[:, g, j, :],
                    rhs=codes[:].bitcast(E4X4),
                    rhs_scale=scales[:],
                    start=True,
                    stop=True,
                )

        def z_step(k):
            ci, g = units[k]
            n, l0 = CHUNKS[ci], starts[ci]
            z = work.tile([P, PACK, n], F32, name="z", tag="z", bufs=3, align_bytes=64)
            for j in range(PACK):
                nc.vector.scalar_tensor_tensor(
                    out=z[:, j, :],
                    in0=st["s1", k, j],
                    scalar=cols_bt[:, j, g : g + 1],
                    in1=t_sb[:, l0 : l0 + n],
                    op0=ADD,
                    op1=MULT,
                )
            st["z", k] = z

        def e_step(k):
            ci, g = units[k]
            n = CHUNKS[ci]
            if k in ASSIST:
                x = work.tile([P, PACK, n], F32, name="xs", tag="x", bufs=3, align_bytes=64)
                nc.scalar.activation(out=x[:], in_=st["z", k][:], func=EXP, scale=0.4)
                y = work.tile([P, PACK, n], BF16, name="y", tag="y", bufs=2, align_bytes=64)
                for j in range(PACK):
                    nc.scalar.activation(
                        out=y[:, j, :],
                        in_=x[:, j, :],
                        func=IDENT,
                        scale=cols_pc[:, j, g : g + 1],
                        bias=minus_p[:, j, g : g + 1],
                    )
                st["x", k] = y
                return
            x = work.tile([P, n * PACK], F32, name="x", tag="x", bufs=3, align_bytes=64)
            step = P if k == len(units) - 1 else n
            for l in range(0, n, step):
                nc.scalar.activation(
                    out=x[:, PACK * l : PACK * (l + step)].rearrange("p (c i t) -> p c t i", i=4, t=PACK),
                    in_=st["z", k][:, :, l : l + step].rearrange("p t (c i) -> p c t i", i=4),
                    func=EXP,
                    scale=0.4,
                )
            st["x", k] = x

        def m_step(k):
            ci, g = units[k]
            n = CHUNKS[ci]
            m = work.tile([P, n * PACK], BF16, name="m", tag="m", bufs=3, align_bytes=64)
            st["m", k] = m
            if k == len(units) - 1:
                for i in range(n // P):
                    part = slice(512 * i, 512 * (i + 1))
                    nc.vector.scalar_tensor_tensor(
                        out=m[:, part].rearrange("p (n t) -> p n t", t=PACK),
                        in0=st["x", k][:, part].rearrange("p (n t) -> p n t", t=PACK),
                        scalar=-1.0,
                        in1=p_sb[:, g, :].unsqueeze(1).to_broadcast([P, P, PACK]),
                        op0=ADD,
                        op1=MULT,
                    )
                return
            if k in ASSIST:
                nc.vector.tensor_copy(
                    out=m[:].rearrange("p (c i t) -> p c t i", i=4, t=PACK),
                    in_=st["x", k][:].rearrange("p t (c i) -> p c t i", i=4),
                )
                return
            nc.vector.scalar_tensor_tensor(
                out=m[:].rearrange("p (n t) -> p n t", t=PACK),
                in0=st["x", k][:].rearrange("p (n t) -> p n t", t=PACK),
                scalar=-1.0,
                in1=p_sb[:, g, :].unsqueeze(1).to_broadcast([P, n, PACK]),
                op0=ADD,
                op1=MULT,
            )

        def q_step(k):
            ci, g = units[k]
            n = CHUNKS[ci]
            if g == 0:
                mc = work.tile([P, GP, n], U32, name="mc", tag="mc", bufs=2, align_bytes=64)
                ms = work.tile([P, GP, n], U8, name="ms", tag="ms", bufs=2, align_bytes=64)
                st["mq", ci] = (mc, ms)
            mc, ms = st["mq", ci]
            step = P if k == len(units) - 1 else n
            for l in range(0, n, step):
                part = slice(l, l + step)
                nc.vector.quantize_mx(
                    out=mc[:, g, part].bitcast(E4X4), scales=ms[:, g, part], in_=st["m", k][:, PACK * l : PACK * (l + step)]
                )

        def mm2(ci, j, passes=range(GP), tag="acc", bufs=2):
            mc, ms = st["mq", ci]
            cols = slice(P * j, P * (j + 1))
            for h in range(QG):
                if 0 in passes:
                    acc = psum.tile([P, 512], F32, name="acc", tag=tag, bufs=bufs)
                    st["acc", ci, j, h] = acc
                acc = st["acc", ci, j, h]
                for g in passes:
                    nc.tensor.matmul_mx(
                        out=acc[:],
                        lhsT=mc[:, g, cols].bitcast(E4X4),
                        lhsT_scale=ms[:, g, cols],
                        rhs=a_sb[:, g, 1024 * h : 1024 * (h + 1)].bitcast(E2X4),
                        rhs_scale=as_sb[:, Q * g + 512 * h : Q * g + 512 * (h + 1)],
                        start=(g == 0),
                        stop=(g == GP - 1),
                    )

        def r_step(ci, j):
            i = starts[ci] // P + j
            r = work.tile([P, Q], F32, name="r", tag="r", bufs=3, align_bytes=64)
            rb = work.tile([P, Q], BF16, name="rb", tag="rb", bufs=3, align_bytes=64)
            kind = KIND[i]
            for h in range(QG):
                half = slice(512 * h, 512 * (h + 1))
                acc = st["acc", ci, j, h]
                if kind == "D" and h == 1:
                    nc.vector.tensor_scalar(
                        out=r[:, half], in0=acc[:], scalar1=cols_pc[:, PACK, 3 + i : 4 + i], scalar2=None, op0=ADD
                    )
                else:
                    nc.scalar.activation(
                        out=r[:, half], in_=acc[:], func=IDENT, bias=cols_pc[:, PACK, 3 + i : 4 + i]
                    )
                if kind == "B":
                    nc.scalar.activation(
                        out=rb[:, half], in_=acc[:], func=IDENT, bias=cols_pc[:, PACK, 3 + i : 4 + i]
                    )
            nc.sync.dma_start(out=out_0[P * i : P * (i + 1), :], in_=r[:])
            st["r", ci, j] = (r, rb, kind)

        def round_step(ci, j):
            r, rb, kind = st["r", ci, j]
            for h in range(QG):
                half = slice(512 * h, 512 * (h + 1))
                if kind == "G":
                    nc.gpsimd.tensor_scalar(
                        out=rb[:, half], in0=r[:, half], scalar1=1.0, scalar2=0.0, op0=MULT, op1=ADD
                    )
                elif kind in "AD":
                    nc.vector.tensor_copy(out=rb[:, half], in_=r[:, half])

        def o_transposes(ci, j):
            r, rb, kind = st["r", ci, j]
            if kind == "C":
                for g in range(QG):
                    tr = psum.tile([P, PACK, P], F32, name="otr", tag="tr", bufs=2)
                    for e in range(PACK):
                        nc.tensor.transpose(tr[:, e, :], r[:, 512 * g + e : 512 * (g + 1) : PACK], ident[:])
                    st["otr", ci, j, g] = tr
                return
            words = rb[:].bitcast(F32)
            tr = psum.tile([P, QG, 2, P], F32, name="otr", tag="tr", bufs=2)
            for g in range(QG):
                for e in range(2):
                    nc.tensor.transpose(tr[:, g, e, :], words[:, 256 * g + e : 256 * (g + 1) : 2], ident[:])
            st["otr", ci, j] = tr

        def o_copy(ci, j):
            n = CHUNKS[ci]
            if j == 0:
                pb = work.tile([P, QG, n * PACK], BF16, name="pb", tag="pb", bufs=2, align_bytes=64)
                st["pb", ci] = pb
            pb = st["pb", ci]
            if st["r", ci, j][2] == "C":
                for g in range(QG):
                    nc.scalar.copy(
                        out=pb[:, g, 512 * j : 512 * (j + 1)].rearrange("p (r t) -> p r t", t=PACK),
                        in_=st["otr", ci, j, g][:].rearrange("p t r -> p r t"),
                    )
                return
            dst = pb[:].rearrange("p g x -> p (g x)").bitcast(F32).rearrange(
                "p (g r e) -> p g r e", g=QG, e=2
            )
            src = st["otr", ci, j][:].rearrange("p g e r -> p g r e")
            here = slice(P * j, P * (j + 1))
            if st["r", ci, j][2] == "D":
                nc.scalar.copy(out=dst[:, 0, here, :], in_=src[:, 0])
                nc.vector.tensor_copy(out=dst[:, 1, here, :], in_=src[:, 1])
            else:
                nc.scalar.copy(out=dst[:, :, here, :], in_=src)

        out_1_v = out_1.rearrange("g p l t -> p g (l t)").bitcast(I32)
        out_2_v = out_2.bitcast(I32)
        pls_v = pl_scales[:].rearrange("p g l -> p (g l)").bitcast(I32).rearrange("p (g l) -> p g l", g=QG)

        def planes(ci):
            n, l0 = CHUNKS[ci], starts[ci]
            pc = work.tile([P, QG * n], U32, name="pc", tag="pc", bufs=2, align_bytes=64)
            for g in range(QG):
                nc.vector.quantize_mx(
                    out=pc[:, g * n : (g + 1) * n].bitcast(E4X4),
                    scales=pl_scales[:, g, l0 : l0 + n],
                    in_=st["pb", ci][:, g, :],
                )
            nc.sync.dma_start(
                out=out_1_v[:, :, l0 : l0 + n],
                in_=pc[:].bitcast(I32).rearrange("p (g n) -> p g n", g=QG),
            )

        def store_scales(l0, l1):
            for q in range(4):
                nc.sync.dma_start(
                    out=out_2_v[:, 4 * q : 4 * q + 4, l0 // 4 : l1 // 4].rearrange("g r l -> r g l"),
                    in_=pls_v[32 * q : 32 * q + 4, :, l0 // 4 : l1 // 4],
                )

        def t_spread(l0, l1, scalar):
            tb = psum.tile([P, l1 - l0], BF16, name="tb", tag="acc", bufs=2)
            for i in range(l0 // P, l1 // P):
                nc.tensor.transpose(
                    tb[:, P * i - l0 : P * (i + 1) - l0], cols_bt[:, PACK, 3 + i : 4 + i].to_broadcast([P, P]), ident_bf[:]
                )
            if scalar:
                nc.scalar.copy(out=t_sb[:, l0:l1], in_=tb[:])
            else:
                nc.vector.tensor_copy(out=t_sb[:, l0:l1], in_=tb[:])

        def columns(rows):
            vec = psum.tile([P, PACK + 1, P], BF16, name="vec", tag="acc", bufs=2)
            for j in range(PACK):
                nc.tensor.transpose(vec[:, j, :], rows[:, j : 512 : PACK], ident_bf[:])
            nc.tensor.transpose(vec[:, PACK, :], rows[:, 0:P], ident_bf[:])
            return vec

        nc.vector.tensor_copy(out=ident_bf[:], in_=ident[:])
        u_transposes(0)
        u_copy(0, False)
        vec_bt = columns(rows_bt)
        nc.scalar.copy(out=cols_bt[:, :, 0:11], in_=vec_bt[:, :, 0:11])
        v_permute(0)
        vs_permute(0)
        u_quant(0)
        t_spread(0, CHUNKS[0], True)
        mm1(0)
        v_permute(1)
        vs_permute(1)
        vec_pc = columns(rows_pc)
        nc.scalar.copy(out=p_sb[:], in_=vec_pc[:, 0:PACK, 0:GP].rearrange("p t g -> p g t"))
        nc.scalar.copy(out=cols_pc[:, :, 0:11], in_=vec_pc[:, :, 0:11])
        nc.scalar.activation(out=minus_p[:], in_=vec_pc[:, 0:PACK, 0:GP], func=IDENT, scale=-1.0)

        n_units = len(units)
        last = len(CHUNKS) - 1
        for k in range(n_units + 2):
            c1, g1 = divmod(k, GP)
            done = (k - 5) // GP
            taking_out = k >= 5 and done < last
            if k + 1 < n_units:
                mm1(k + 1)
            if g1 == 0 and c1 + 1 < len(CHUNKS):
                u_transposes(c1 + 1)
            if 0 <= k - 1 < n_units:
                e_step(k - 1)
            if k == 1:
                u_copy(1, False)
                t_spread(CHUNKS[0], L, True)
            if g1 == 1 and 0 < c1 and c1 + 1 < len(CHUNKS):
                u_copy(c1 + 1, False)
            if taking_out and g1 == 2:
                r_step(done, 0)
            if taking_out and g1 == 0:
                r_step(done, 1)
            if 0 <= k - 2 < n_units:
                m_step(k - 2)
            if k < n_units:
                z_step(k)
            if k == 0:
                v_permute(2)
                vs_permute(2)
            if 0 <= k - 2 < n_units:
                q_step(k - 2)
            if g1 == 1 and c1 + 1 < len(CHUNKS):
                u_quant(c1 + 1)
            if taking_out and g1 == 2:
                round_step(done, 0)
            if taking_out and g1 == 0:
                round_step(done, 1)
            if g1 == 0 and k >= 9:
                planes(k // GP - 3)
            if taking_out and g1 == 0:
                o_transposes(done, 0)
                o_copy(done, 0)
            if taking_out and g1 == 1:
                o_transposes(done, 1)
                o_copy(done, 1)
            if k >= 4 and (k - 4) // GP < last and g1 > 0:
                mm2((k - 4) // GP, g1 - 1)
            if k == n_units:
                for j in range(2):
                    mm2(last, j, range(0, 2), "s1", 4)

        store_scales(0, starts[-2])
        for j in range(2):
            mm2(last, j, range(2, 3))
        for j in range(2):
            r_step(last, j)
            round_step(last, j)
            o_transposes(last, j)
        planes(last - 1)
        store_scales(starts[-2], starts[-1])
        for j in range(2):
            o_copy(last, j)
        planes(last)
        store_scales(starts[-1], L)
